import numpy as np
import ml_dtypes


def mxq(x, axis, fmt="e4m3"):
    dtype, down = {"e4m3": (ml_dtypes.float8_e4m3fn, 7), "e5m2": (ml_dtypes.float8_e5m2, 14)}[fmt]
    v = np.moveaxis(np.asarray(x, np.float32).astype(ml_dtypes.bfloat16).astype(np.float64), axis, -1)
    blocks = v.reshape(v.shape[:-1] + (-1, 32))
    amax = np.abs(blocks).max(-1, keepdims=True)
    byte = np.maximum(np.where(amax > 0, np.frexp(amax)[1] - 1 + 127, 0) - down, 1)
    scale = np.exp2(byte - 127.0)
    codes = (blocks / scale).astype(np.float32).astype(dtype).astype(np.float64)
    return np.moveaxis((codes * scale).reshape(v.shape), -1, axis)


WIDE = False


def mx_kscale(k):
    if not WIDE:
        return np.ones(k)
    levels = np.array([10, -10, 5, -5, 0])
    if k % 512:
        return np.exp2(np.random.permutation(np.resize(levels, k // 32))).repeat(32)
    a = np.empty((k // 512, 16))
    for p in range(k // 512):
        a[p, :8] = np.random.permutation(np.resize(levels, 8))
        for g in range(8):
            far = levels[np.abs(levels - a[p, g]) >= 10]
            a[p, g + 8] = far[np.random.randint(len(far))]
    return np.exp2(a.ravel()).repeat(32)


def f64(x):
    return np.asarray(x).astype(np.float64)


def striped(idx):
    return np.tile(idx.reshape(-1, 16).T, (8, 1)).astype(np.uint16)


def unstriped(offs):
    return offs[:16].T.reshape(-1).astype(np.int64)


K, T, E, C, N = 512, 768, 12, 256, 128
TOP = 4
M = 512


def by_expert(wq, xq):
    return np.concatenate([wq[e].T @ xq[:, e * C:(e + 1) * C] for e in range(E)], axis=1)


def setup_inputs():
    n = np.random.standard_normal
    s = mx_kscale(K)[:, None]
    deal = np.repeat(np.arange(E), C).reshape(TOP, T)[:, np.random.permutation(T)]
    deal = np.take_along_axis(deal, np.argsort(np.random.rand(TOP, T), axis=0), axis=0)
    for _ in range(8):
        s_, t_ = np.random.permutation(T).reshape(2, -1); r = np.random.randint(TOP, size=T // 2); x, y = deal[r, s_].copy(), deal[r, t_].copy()
        ok = ~((deal[:, s_] == y).any(0) | (deal[:, t_] == x).any(0)); deal[r[ok], s_[ok]] = y[ok]; deal[r[ok], t_[ok]] = x[ok]
    order = np.lexsort((np.random.rand(TOP * T), deal.reshape(-1)))
    slot_token = order % T; pos = np.empty(TOP * T, np.int64); pos[order] = np.arange(TOP * T); pos = pos.reshape(TOP, T)
    g = np.random.uniform(0.5, 1.5, (TOP, T)); g = g / g.sum(0)
    r = mx_kscale(M)[:, None]
    return {
        "uT": (n((M, T)) * r).astype(np.float32),
        "wu": (n((M, K)) / np.sqrt(M) / r * s.T).astype(np.float32),
        "w": (n((E, K, N)) / np.sqrt(K) / s[None]).astype(np.float32),
        "gate": np.stack([np.tile(r, (N, 1)) for r in g]).astype(np.float32),
        "offs": striped(slot_token),
        "pos1": striped(pos[0]),
        "pos2": striped(pos[1]),
        "pos3": striped(pos[2]),
        "pos4": striped(pos[3]),
    }


def reference(uT, wu, w, gate, offs, pos1, pos2, pos3, pos4):
    idx = unstriped(offs)
    x = mxq(f64(wu), 0, "e4m3").T @ mxq(f64(uT), 0, "e4m3")
    xq = mxq(x[:, idx], 0, "e4m3")
    y = by_expert(mxq(f64(w), 1, "e4m3"), xq)
    return sum(f64(gate[r]) * y[:, unstriped(p)] for r, p in enumerate((pos1, pos2, pos3, pos4)))

@@ -1,0 +1,230 @@
+from contextlib import ExitStack
+
+import concourse.mybir as mybir
+from concourse.masks import make_identity
+
+K, T, E, C, N, M = 512, 768, 12, 256, 128, 512
+TOP = 4
+S = E * C
+
+FLOPS = 2 * M * K * T + 2 * K * N * S
+
+F32 = mybir.dt.float32
+BF16 = mybir.dt.bfloat16
+U32 = mybir.dt.uint32
+U16 = mybir.dt.uint16
+U8 = mybir.dt.uint8
+FP8X4 = mybir.dt.float8_e4m3fn_x4
+COPY = mybir.ActivationFunctionType.Copy
+MULT = mybir.AluOpType.mult
+ADD = mybir.AluOpType.add
+
+P = 128
+PACK = 4
+TOKEN_CHUNKS = (128, 256, 256, 128)
+SLOT_CHUNKS = (512, 512, 512, 512, 512, 256, 128, 128)
+HALF = T // 2
+BLOCKS = HALF // P
+
+
+def starts(widths):
+    return [sum(widths[:i]) for i in range(len(widths))]
+
+
+def tile_moe_prv_lin_none_kernel(tc, uT, wu, w, gate, offs, pos1, pos2, pos3, pos4, out):
+    nc = tc.nc
+    with ExitStack() as ctx:
+        lists = ctx.enter_context(tc.tile_pool(name="lists", bufs=1))
+        keep = ctx.enter_context(tc.tile_pool(name="keep", bufs=1))
+        ring = ctx.enter_context(tc.tile_pool(name="ring", bufs=2))
+        banks = ctx.enter_context(tc.psum_pool(name="banks", bufs=6))
+        sums = ctx.enter_context(tc.psum_pool(name="sums", bufs=2))
+
+        def quantize(pool, grouped, width, name, tag=""):
+            codes = pool.tile([P, width], U32, name=name + "_codes", tag=tag, align_bytes=64)
+            scales = pool.tile([P, width], U8, name=name + "_scales", align_bytes=64)
+            nc.vector.quantize_mx(out=codes[:].bitcast(FP8X4), scales=scales[:], in_=grouped)
+            return codes, scales
+
+        def multiply(result, stationary, m_cols, moving, n_cols):
+            nc.tensor.matmul_mx(
+                out=result,
+                lhsT=stationary[0][:, m_cols].bitcast(FP8X4),
+                lhsT_scale=stationary[1][:, m_cols],
+                rhs=moving[0][:, n_cols].bitcast(FP8X4),
+                rhs_scale=moving[1][:, n_cols],
+                start=True,
+                stop=True,
+            )
+
+        wu_raw = []
+        for h in range(2):
+            raw = keep.tile([P, PACK, K // 2], F32, name=f"wu_raw{h}")
+            nc.sync.dma_start(out=raw[:], in_=wu[:, h * (K // 2):(h + 1) * (K // 2)].rearrange("(p j) c -> p j c", j=PACK))
+            wu_raw.append(raw)
+        u_raw = []
+        for t0, width in zip(starts(TOKEN_CHUNKS), TOKEN_CHUNKS):
+            raw = keep.tile([P, PACK, width], F32, name=f"u_raw{t0}")
+            nc.sync.dma_start(out=raw[:], in_=uT[:, t0:t0 + width].rearrange("(p j) c -> p j c", j=PACK))
+            u_raw.append(raw)
+        offs_sb = lists.tile([P, S // 16], U16, name="offs_sb")
+        nc.sync.dma_start(offs_sb[:], offs)
+        w_raw = []
+        for q in range(E // 2):
+            raw = keep.tile([P, 2, PACK * N], F32, name=f"w_raw{q}")
+            nc.sync.dma_start(out=raw[:], in_=w[2 * q:2 * q + 2].rearrange("e (p j) n -> p e (j n)", j=PACK))
+            w_raw.append(raw)
+        pos_sb = []
+        for r, pos in enumerate((pos1, pos2, pos3, pos4)):
+            tile = lists.tile([P, T // 16], U16, name=f"pos_sb{r}")
+            nc.sync.dma_start(tile[:], pos)
+            pos_sb.append(tile)
+        gate_last = keep.tile([P, T], F32, name="gate_last")
+        nc.sync.dma_start(out=gate_last[:], in_=gate[TOP - 1])
+        ident = keep.tile([P, P], F32, name="ident")
+        make_identity(nc, ident[:])
+        gate_rows = keep.tile([P, TOP - 1, P], F32, name="gate_rows")
+        nc.gpsimd.memset(gate_rows[:], 0.0)
+        nc.sync.dma_start(out=gate_rows[0:T // P, :, :], in_=gate[0:TOP - 1, 0, :].rearrange("r (c t) -> c r t", t=P))
+
+        wu_grouped = keep.tile([P, K * PACK], BF16, name="wu_grouped", tag="staged", align_bytes=64)
+        wu_view = wu_grouped[:].rearrange("p (t m j) -> p m t j", t=PACK, j=PACK)
+        wu_from = [raw[:].rearrange("p j (m t) -> p m t j", t=PACK) for raw in wu_raw]
+        for h in range(2):
+            nc.vector.tensor_copy(wu_view[:, 64 * h:64 * h + 32], wu_from[h][:, 0:32])
+            nc.scalar.activation(wu_view[:, 64 * h + 32:64 * h + 64], wu_from[h][:, 32:64], COPY)
+        wu_mx = quantize(keep, wu_grouped[:], K, "wu")
+
+        x_pairs = [keep.tile([P, 2 * T], BF16, name=f"x_pairs{u}", align_bytes=64) for u in range(2)]
+        token_starts = starts(TOKEN_CHUNKS)
+
+        def cast_tokens(i, copies):
+            width = TOKEN_CHUNKS[i]
+            grouped = keep.tile([P, width * PACK], BF16, name=f"u_grouped{i}", tag="staged" if i in (1, 2) else "", align_bytes=64)
+            to_view = grouped[:].rearrange("p (c i j) -> p c j i", i=4, j=PACK)
+            from_view = u_raw[i][:].rearrange("p j (c i) -> p c j i", i=4)
+            share = width // 4 // len(copies)
+            for n, copy in enumerate(copies):
+                copy(to_view[:, n * share:(n + 1) * share], from_view[:, n * share:(n + 1) * share])
+            return grouped
+
+        def project(i, u_mx, u, copy):
+            t0, width = token_starts[i], TOKEN_CHUNKS[i]
+            bank = banks.tile([P, 2, width], F32, name="bank")
+            for e in range(2):
+                j = 2 * u + e
+                multiply(bank[:, e, :], wu_mx, slice(j * P, (j + 1) * P), u_mx, slice(0, width))
+            copy(
+                x_pairs[u][:, 2 * t0:2 * (t0 + width)].rearrange("p (t e) -> p t e", e=2),
+                bank[:].rearrange("p e t -> p t e"),
+            )
+
+        on_vector, on_scalar = nc.vector.tensor_copy, nc.scalar.copy
+        g0 = cast_tokens(0, [on_scalar])
+        mx0 = quantize(keep, g0[:], TOKEN_CHUNKS[0], "u0")
+        g1 = cast_tokens(1, [on_vector, on_scalar])
+        mx1 = quantize(keep, g1[:], TOKEN_CHUNKS[1], "u1")
+        project(0, mx0, 0, on_scalar)
+        project(0, mx0, 1, on_scalar)
+        g2 = cast_tokens(2, [on_vector, on_scalar])
+        g3 = cast_tokens(3, [on_vector])
+        mx2 = quantize(keep, g2[:], TOKEN_CHUNKS[2], "u2")
+        mx3 = quantize(keep, g3[:], TOKEN_CHUNKS[3], "u3", tag="late")
+        project(1, mx1, 0, on_scalar)
+        project(1, mx1, 1, on_scalar)
+        project(2, mx2, 0, on_vector)
+        project(3, mx3, 0, on_scalar)
+        project(2, mx2, 1, on_scalar)
+        project(3, mx3, 1, on_scalar)
+
+        y = keep.tile([P, S], F32, name="y")
+        w_grouped = {}
+        w_mx = {}
+
+        def cast_weights(q):
+            grouped = keep.tile([P, 2 * N * PACK], BF16, name=f"w_grouped{q}", tag="late" if q == 0 else "", align_bytes=64)
+            nc.scalar.copy(
+                grouped[:].rearrange("p (e c i j) -> p e c j i", e=2, i=4, j=PACK),
+                w_raw[q][:].rearrange("p e (j c i) -> p e c j i", j=PACK, i=4),
+            )
+            w_grouped[q] = grouped
+
+        def gather_slots(s0, width):
+            planes = ring.tile([P, 2, width], U32, name="planes")
+            for u in range(2):
+                nc.vector.tensor_copy(
+                    planes[:, u, :],
+                    x_pairs[u][:].bitcast(U32).indirect(offs_sb[:, s0 // 16:(s0 + width) // 16]),
+                )
+            grouped = ring.tile([P, width * PACK], BF16, name="x_grouped", align_bytes=64)
+            nc.scalar.copy(
+                grouped[:].bitcast(U32).rearrange("p (s u) -> p s u", u=2),
+                planes[:].rearrange("p u s -> p s u"),
+            )
+            return grouped
+
+        def gather_slots_stepped(s0, width):
+            grouped = ring.tile([P, width * PACK], BF16, name="x_grouped", align_bytes=64)
+            words = grouped[:].bitcast(U32).rearrange("p (s u) -> p s u", u=2)
+            for u in range(2):
+                nc.vector.tensor_copy(
+                    words[:, :, u],
+                    x_pairs[u][:].bitcast(U32).indirect(offs_sb[:, s0 // 16:(s0 + width) // 16]),
+                )
+            return grouped
+
+        def run_experts(grouped, s0, width):
+            q = s0 // (2 * C)
+            if q not in w_mx:
+                w_mx[q] = quantize(keep, w_grouped[q][:], 2 * N, f"w{q}")
+            x_mx = quantize(ring, grouped[:], width, "x")
+            bank = banks.tile([P, width], F32, name="bank")
+            step = min(C, width)
+            for c0 in range(0, width, step):
+                e = (s0 + c0) // C - 2 * q
+                multiply(bank[:, c0:c0 + step], w_mx[q], slice(e * N, (e + 1) * N), x_mx, slice(c0, c0 + step))
+            nc.scalar.copy(y[:, s0:s0 + width], bank[:])
+
+        cast_weights(0)
+        waiting = None
+        for s0, width in zip(starts(SLOT_CHUNKS), SLOT_CHUNKS):
+            grouped = (gather_slots if s0 + width < S else gather_slots_stepped)(s0, width)
+            if waiting is not None:
+                run_experts(*waiting)
+            q_next = (s0 + width) // (2 * C)
+            if q_next < E // 2 and q_next not in w_grouped:
+                cast_weights(q_next)
+            waiting = (grouped, s0, width)
+        run_experts(*waiting)
+
+        gate_bank = banks.tile([P, TOP - 1, P], F32, name="bank")
+        for r in range(TOP - 1):
+            nc.tensor.transpose(gate_bank[:, r, :], gate_rows[:, r, :], ident[:])
+        gate_cols = keep.tile([P, TOP - 1, T // P], F32, name="gate_cols")
+        nc.scalar.copy(gate_cols[:], gate_bank[:, :, 0:T // P])
+
+        partial = []
+        for h in range(2):
+            entries = slice(h * HALF // 16, (h + 1) * HALF // 16)
+            total = sums.tile([P, HALF], F32, name="total")
+            for r in range(TOP - 1):
+                picked = keep.tile([P, HALF], F32, name=f"picked{h}_{r}")
+                nc.vector.tensor_copy(picked[:], y[:].indirect(pos_sb[r][:, entries]))
+                turned = banks.tile([P, BLOCKS, P], F32, name="bank")
+                for b in range(BLOCKS):
+                    nc.tensor.transpose(turned[:, b, :], picked[:, b * P:(b + 1) * P], ident[:])
+                scaled = keep.tile([P, BLOCKS, P], F32, name=f"scaled{h}_{r}")
+                for b in range(BLOCKS):
+                    c = h * BLOCKS + b
+                    nc.scalar.activation(scaled[:, b, :], turned[:, b, :], COPY, scale=gate_cols[:, r, c:c + 1])
+                for b in range(BLOCKS):
+                    nc.tensor.matmul(total[:, b * P:(b + 1) * P], scaled[:, b, :], ident[:],
+                                     start=(r == 0 and b == 0), stop=(r == TOP - 2 and b == BLOCKS - 1), is_transpose=True)
+            partial.append(total)
+        last = keep.tile([P, T], F32, name="last")
+        nc.vector.tensor_tensor(last[:], y[:].indirect(pos_sb[TOP - 1][:]), gate_last[:], MULT)
+        for h in range(2):
+            cols = slice(h * HALF, (h + 1) * HALF)
+            result = keep.tile([P, HALF], F32, name=f"result{h}")
+            nc.vector.tensor_tensor(result[:], partial[h][:], last[:, cols], ADD)
+            nc.sync.dma_start(out=out[:, cols], in_=result[:])

@@ -21,7 +21,7 @@ ADD = mybir.AluOpType.add
 
 P = 128
 PACK = 4
-TOKEN_CHUNKS = (128, 256, 256, 128)
+TOKEN_CHUNKS = (128, 256, 128, 128, 128)
 SLOT_CHUNKS = (512, 512, 512, 512, 512, 256, 128, 128)
 HALF = T // 2
 BLOCKS = HALF // P
@@ -37,7 +37,7 @@ def tile_moe_prv_lin_none_kernel(tc, uT, wu, w, gate, offs, pos1, pos2, pos3, po
         lists = ctx.enter_context(tc.tile_pool(name="lists", bufs=1))
         keep = ctx.enter_context(tc.tile_pool(name="keep", bufs=1))
         ring = ctx.enter_context(tc.tile_pool(name="ring", bufs=2))
-        banks = ctx.enter_context(tc.psum_pool(name="banks", bufs=6))
+        banks = ctx.enter_context(tc.psum_pool(name="banks", bufs=5))
         sums = ctx.enter_context(tc.psum_pool(name="sums", bufs=2))
 
         def quantize(pool, grouped, width, name, tag=""):
@@ -98,9 +98,9 @@ def tile_moe_prv_lin_none_kernel(tc, uT, wu, w, gate, offs, pos1, pos2, pos3, po
         x_pairs = [keep.tile([P, 2 * T], BF16, name=f"x_pairs{u}", align_bytes=64) for u in range(2)]
         token_starts = starts(TOKEN_CHUNKS)
 
-        def cast_tokens(i, copies):
+        def cast_tokens(i, copies, tag):
             width = TOKEN_CHUNKS[i]
-            grouped = keep.tile([P, width * PACK], BF16, name=f"u_grouped{i}", tag="staged" if i in (1, 2) else "", align_bytes=64)
+            grouped = keep.tile([P, width * PACK], BF16, name=f"u_grouped{i}", tag=tag, align_bytes=64)
             to_view = grouped[:].rearrange("p (c i j) -> p c j i", i=4, j=PACK)
             from_view = u_raw[i][:].rearrange("p j (c i) -> p c j i", i=4)
             share = width // 4 // len(copies)
@@ -108,9 +108,9 @@ def tile_moe_prv_lin_none_kernel(tc, uT, wu, w, gate, offs, pos1, pos2, pos3, po
                 copy(to_view[:, n * share:(n + 1) * share], from_view[:, n * share:(n + 1) * share])
             return grouped
 
-        def project(i, u_mx, u, copy):
+        def project(i, u_mx, u, copy, held=False):
             t0, width = token_starts[i], TOKEN_CHUNKS[i]
-            bank = banks.tile([P, 2, width], F32, name="bank")
+            bank = banks.tile([P, 2, width], F32, name="held" if held else "bank", bufs=1 if held else 5)
             for e in range(2):
                 j = 2 * u + e
                 multiply(bank[:, e, :], wu_mx, slice(j * P, (j + 1) * P), u_mx, slice(0, width))
@@ -120,32 +120,37 @@ def tile_moe_prv_lin_none_kernel(tc, uT, wu, w, gate, offs, pos1, pos2, pos3, po
             )
 
         on_vector, on_scalar = nc.vector.tensor_copy, nc.scalar.copy
-        g0 = cast_tokens(0, [on_scalar])
+        g0 = cast_tokens(0, [on_scalar], "staged2")
         mx0 = quantize(keep, g0[:], TOKEN_CHUNKS[0], "u0")
-        g1 = cast_tokens(1, [on_vector, on_scalar])
-        mx1 = quantize(keep, g1[:], TOKEN_CHUNKS[1], "u1")
         project(0, mx0, 0, on_scalar)
+        g1 = cast_tokens(1, [on_vector, on_scalar], "staged")
+        g2 = cast_tokens(2, [on_vector], "staged2")
+        mx1 = quantize(keep, g1[:], TOKEN_CHUNKS[1], "u1")
         project(0, mx0, 1, on_scalar)
-        g2 = cast_tokens(2, [on_vector, on_scalar])
-        g3 = cast_tokens(3, [on_vector])
+        g3 = cast_tokens(3, [on_vector], "")
         mx2 = quantize(keep, g2[:], TOKEN_CHUNKS[2], "u2")
-        mx3 = quantize(keep, g3[:], TOKEN_CHUNKS[3], "u3", tag="late")
+        g4 = cast_tokens(4, [on_vector], "staged")
+        mx3 = quantize(keep, g3[:], TOKEN_CHUNKS[3], "u3")
+        mx4 = quantize(keep, g4[:], TOKEN_CHUNKS[4], "u4", tag="late")
         project(1, mx1, 0, on_scalar)
-        project(1, mx1, 1, on_scalar)
-        project(2, mx2, 0, on_vector)
-        project(3, mx3, 0, on_scalar)
+        project(2, mx2, 0, on_scalar, held=True)
+        project(3, mx3, 0, on_vector)
+        project(4, mx4, 0, on_vector)
+        project(1, mx1, 1, on_scalar, held=True)
         project(2, mx2, 1, on_scalar)
         project(3, mx3, 1, on_scalar)
+        project(4, mx4, 1, on_scalar)
 
         y = keep.tile([P, S], F32, name="y")
         w_grouped = {}
         w_mx = {}
 
         def cast_weights(q):
-            grouped = keep.tile([P, 2 * N * PACK], BF16, name=f"w_grouped{q}", tag="late" if q == 0 else "", align_bytes=64)
-            nc.scalar.copy(
-                grouped[:].rearrange("p (e c i j) -> p e c j i", e=2, i=4, j=PACK),
-                w_raw[q][:].rearrange("p e (j c i) -> p e c j i", j=PACK, i=4),
+            grouped = keep.tile([P, 2 * N * PACK], BF16, name=f"w_grouped{q}", tag="late", align_bytes=64)
+            nc.gpsimd.tensor_scalar(
+                grouped[:].rearrange("p (e n j) -> p e n j", e=2, j=PACK),
+                w_raw[q][:].rearrange("p e (j n) -> p e n j", j=PACK),
+                1.0, 0.0, MULT, ADD,
             )
             w_grouped[q] = grouped
 
@@ -191,9 +196,9 @@ def tile_moe_prv_lin_none_kernel(tc, uT, wu, w, gate, offs, pos1, pos2, pos3, po
             grouped = (gather_slots if s0 + width < S else gather_slots_stepped)(s0, width)
             if waiting is not None:
                 run_experts(*waiting)
-            q_next = (s0 + width) // (2 * C)
-            if q_next < E // 2 and q_next not in w_grouped:
-                cast_weights(q_next)
+            q_now = s0 // (2 * C)
+            if q_now not in w_grouped:
+                cast_weights(q_now)
             waiting = (grouped, s0, width)
         run_experts(*waiting)
 

@@ -21,7 +21,7 @@ ADD = mybir.AluOpType.add
 
 P = 128
 PACK = 4
-TOKEN_CHUNKS = (128, 256, 128, 128, 128)
+TOKEN_CHUNKS = (256, 256, 256)
 SLOT_CHUNKS = (512, 512, 512, 512, 512, 256, 128, 128)
 HALF = T // 2
 BLOCKS = HALF // P
@@ -37,8 +37,9 @@ def tile_moe_prv_lin_none_kernel(tc, uT, wu, w, gate, offs, pos1, pos2, pos3, po
         lists = ctx.enter_context(tc.tile_pool(name="lists", bufs=1))
         keep = ctx.enter_context(tc.tile_pool(name="keep", bufs=1))
         ring = ctx.enter_context(tc.tile_pool(name="ring", bufs=2))
-        banks = ctx.enter_context(tc.psum_pool(name="banks", bufs=5))
+        banks = ctx.enter_context(tc.psum_pool(name="banks", bufs=4))
         sums = ctx.enter_context(tc.psum_pool(name="sums", bufs=2))
+        turns = ctx.enter_context(tc.psum_pool(name="turns", bufs=2))
 
         def quantize(pool, grouped, width, name, tag=""):
             codes = pool.tile([P, width], U32, name=name + "_codes", tag=tag, align_bytes=64)
@@ -57,11 +58,8 @@ def tile_moe_prv_lin_none_kernel(tc, uT, wu, w, gate, offs, pos1, pos2, pos3, po
                 stop=True,
             )
 
-        wu_raw = []
-        for h in range(2):
-            raw = keep.tile([P, PACK, K // 2], F32, name=f"wu_raw{h}")
-            nc.sync.dma_start(out=raw[:], in_=wu[:, h * (K // 2):(h + 1) * (K // 2)].rearrange("(p j) c -> p j c", j=PACK))
-            wu_raw.append(raw)
+        wu_raw = keep.tile([P, PACK, K], F32, name="wu_raw")
+        nc.sync.dma_start(out=wu_raw[:], in_=wu.rearrange("(p j) c -> p j c", j=PACK))
         u_raw = []
         for t0, width in zip(starts(TOKEN_CHUNKS), TOKEN_CHUNKS):
             raw = keep.tile([P, PACK, width], F32, name=f"u_raw{t0}")
@@ -89,28 +87,26 @@ def tile_moe_prv_lin_none_kernel(tc, uT, wu, w, gate, offs, pos1, pos2, pos3, po
 
         wu_grouped = keep.tile([P, K * PACK], BF16, name="wu_grouped", tag="staged", align_bytes=64)
         wu_view = wu_grouped[:].rearrange("p (t m j) -> p m t j", t=PACK, j=PACK)
-        wu_from = [raw[:].rearrange("p j (m t) -> p m t j", t=PACK) for raw in wu_raw]
-        for h in range(2):
-            nc.vector.tensor_copy(wu_view[:, 64 * h:64 * h + 32], wu_from[h][:, 0:32])
-            nc.scalar.activation(wu_view[:, 64 * h + 32:64 * h + 64], wu_from[h][:, 32:64], COPY)
+        wu_from = wu_raw[:].rearrange("p j (m t) -> p m t j", t=PACK)
+        nc.vector.tensor_copy(wu_view[:, 0:64], wu_from[:, 0:64])
+        nc.scalar.activation(wu_view[:, 64:128], wu_from[:, 64:128], COPY)
         wu_mx = quantize(keep, wu_grouped[:], K, "wu")
 
         x_pairs = [keep.tile([P, 2 * T], BF16, name=f"x_pairs{u}", align_bytes=64) for u in range(2)]
-        token_starts = starts(TOKEN_CHUNKS)
+        on_vector, on_scalar = nc.vector.tensor_copy, nc.scalar.copy
 
-        def cast_tokens(i, copies, tag):
-            width = TOKEN_CHUNKS[i]
-            grouped = keep.tile([P, width * PACK], BF16, name=f"u_grouped{i}", tag=tag, align_bytes=64)
+        def cast_tokens(t0, width, copies, tag):
+            raw, c0 = u_raw[t0 // 256], t0 % 256
+            grouped = keep.tile([P, width * PACK], BF16, name=f"u_grouped{t0}", tag=tag, align_bytes=64)
             to_view = grouped[:].rearrange("p (c i j) -> p c j i", i=4, j=PACK)
-            from_view = u_raw[i][:].rearrange("p j (c i) -> p c j i", i=4)
+            from_view = raw[:, :, c0:c0 + width].rearrange("p j (c i) -> p c j i", i=4)
             share = width // 4 // len(copies)
             for n, copy in enumerate(copies):
                 copy(to_view[:, n * share:(n + 1) * share], from_view[:, n * share:(n + 1) * share])
             return grouped
 
-        def project(i, u_mx, u, copy, held=False):
-            t0, width = token_starts[i], TOKEN_CHUNKS[i]
-            bank = banks.tile([P, 2, width], F32, name="held" if held else "bank", bufs=1 if held else 5)
+        def project(t0, width, u_mx, u, copy):
+            bank = banks.tile([P, 2, width], F32, name="bank")
             for e in range(2):
                 j = 2 * u + e
                 multiply(bank[:, e, :], wu_mx, slice(j * P, (j + 1) * P), u_mx, slice(0, width))
@@ -119,38 +115,29 @@ def tile_moe_prv_lin_none_kernel(tc, uT, wu, w, gate, offs, pos1, pos2, pos3, po
                 bank[:].rearrange("p e t -> p t e"),
             )
 
-        on_vector, on_scalar = nc.vector.tensor_copy, nc.scalar.copy
-        g0 = cast_tokens(0, [on_scalar], "staged2")
-        mx0 = quantize(keep, g0[:], TOKEN_CHUNKS[0], "u0")
-        project(0, mx0, 0, on_scalar)
-        g1 = cast_tokens(1, [on_vector, on_scalar], "staged")
-        g2 = cast_tokens(2, [on_vector], "staged2")
-        mx1 = quantize(keep, g1[:], TOKEN_CHUNKS[1], "u1")
-        project(0, mx0, 1, on_scalar)
-        g3 = cast_tokens(3, [on_vector], "")
-        mx2 = quantize(keep, g2[:], TOKEN_CHUNKS[2], "u2")
-        g4 = cast_tokens(4, [on_vector], "staged")
-        mx3 = quantize(keep, g3[:], TOKEN_CHUNKS[3], "u3")
-        mx4 = quantize(keep, g4[:], TOKEN_CHUNKS[4], "u4", tag="late")
-        project(1, mx1, 0, on_scalar)
-        project(2, mx2, 0, on_scalar, held=True)
-        project(3, mx3, 0, on_vector)
-        project(4, mx4, 0, on_vector)
-        project(1, mx1, 1, on_scalar, held=True)
-        project(2, mx2, 1, on_scalar)
-        project(3, mx3, 1, on_scalar)
-        project(4, mx4, 1, on_scalar)
+        g0 = cast_tokens(0, 256, [on_scalar], "staged2")
+        g1 = cast_tokens(256, 256, [on_vector, on_scalar], "staged")
+        mx0 = quantize(keep, g0[:], 256, "u0")
+        g2 = cast_tokens(512, 128, [on_scalar], "staged2")
+        mx1 = quantize(keep, g1[:], 256, "u1")
+        g3 = cast_tokens(640, 128, [on_vector], "staged")
+        mx2 = quantize(keep, g2[:], 128, "u2")
+        mx3 = quantize(keep, g3[:], 128, "u3", tag="late")
+        pieces = ((0, 256, mx0), (256, 256, mx1), (512, 128, mx2), (640, 128, mx3))
+        for piece, copy in zip(pieces, (on_scalar, on_scalar, on_vector, on_vector)):
+            project(*piece, 0, copy)
+        for piece in pieces:
+            project(*piece, 1, on_scalar)
 
         y = keep.tile([P, S], F32, name="y")
         w_grouped = {}
         w_mx = {}
 
         def cast_weights(q):
-            grouped = keep.tile([P, 2 * N * PACK], BF16, name=f"w_grouped{q}", tag="late", align_bytes=64)
-            nc.gpsimd.tensor_scalar(
-                grouped[:].rearrange("p (e n j) -> p e n j", e=2, j=PACK),
-                w_raw[q][:].rearrange("p e (j n) -> p e n j", j=PACK),
-                1.0, 0.0, MULT, ADD,
+            grouped = keep.tile([P, 2 * N * PACK], BF16, name=f"w_grouped{q}", tag="late" if q == 0 else "", align_bytes=64)
+            nc.scalar.copy(
+                grouped[:].rearrange("p (e c i j) -> p e c j i", e=2, i=4, j=PACK),
+                w_raw[q][:].rearrange("p e (j c i) -> p e c j i", j=PACK, i=4),
             )
             w_grouped[q] = grouped
 
@@ -194,11 +181,11 @@ def tile_moe_prv_lin_none_kernel(tc, uT, wu, w, gate, offs, pos1, pos2, pos3, po
         waiting = None
         for s0, width in zip(starts(SLOT_CHUNKS), SLOT_CHUNKS):
             grouped = (gather_slots if s0 + width < S else gather_slots_stepped)(s0, width)
+            q_next = (s0 + width) // (2 * C)
+            if q_next < E // 2 and q_next not in w_grouped:
+                cast_weights(q_next)
             if waiting is not None:
                 run_experts(*waiting)
-            q_now = s0 // (2 * C)
-            if q_now not in w_grouped:
-                cast_weights(q_now)
             waiting = (grouped, s0, width)
         run_experts(*waiting)
 
@@ -208,24 +195,33 @@ def tile_moe_prv_lin_none_kernel(tc, uT, wu, w, gate, offs, pos1, pos2, pos3, po
         gate_cols = keep.tile([P, TOP - 1, T // P], F32, name="gate_cols")
         nc.scalar.copy(gate_cols[:], gate_bank[:, :, 0:T // P])
 
-        partial = []
+        partial = [sums.tile([P, HALF], F32, name="total") for h in range(2)]
+
+        def pick_and_scale(h, r):
+            picked = keep.tile([P, HALF], F32, name=f"picked{h}_{r}")
+            nc.vector.tensor_copy(picked[:], y[:].indirect(pos_sb[r][:, h * HALF // 16:(h + 1) * HALF // 16]))
+            turned = turns.tile([P, BLOCKS, P], F32, name="turned")
+            for b in range(BLOCKS):
+                nc.tensor.transpose(turned[:, b, :], picked[:, b * P:(b + 1) * P], ident[:])
+            scaled = keep.tile([P, BLOCKS, P], F32, name=f"scaled{h}_{r}")
+            for b in range(BLOCKS):
+                c = h * BLOCKS + b
+                nc.scalar.activation(scaled[:, b, :], turned[:, b, :], COPY, scale=gate_cols[:, r, c:c + 1])
+            return scaled
+
+        def add_up(h, r, scaled):
+            for b in range(BLOCKS):
+                nc.tensor.matmul(partial[h][:, b * P:(b + 1) * P], scaled[:, b, :], ident[:],
+                                 start=(r == 0 and b == 0), stop=(r == TOP - 2 and b == BLOCKS - 1), is_transpose=True)
+
+        behind = None
         for h in range(2):
-            entries = slice(h * HALF // 16, (h + 1) * HALF // 16)
-            total = sums.tile([P, HALF], F32, name="total")
             for r in range(TOP - 1):
-                picked = keep.tile([P, HALF], F32, name=f"picked{h}_{r}")
-                nc.vector.tensor_copy(picked[:], y[:].indirect(pos_sb[r][:, entries]))
-                turned = banks.tile([P, BLOCKS, P], F32, name="bank")
-                for b in range(BLOCKS):
-                    nc.tensor.transpose(turned[:, b, :], picked[:, b * P:(b + 1) * P], ident[:])
-                scaled = keep.tile([P, BLOCKS, P], F32, name=f"scaled{h}_{r}")
-                for b in range(BLOCKS):
-                    c = h * BLOCKS + b
-                    nc.scalar.activation(scaled[:, b, :], turned[:, b, :], COPY, scale=gate_cols[:, r, c:c + 1])
-                for b in range(BLOCKS):
-                    nc.tensor.matmul(total[:, b * P:(b + 1) * P], scaled[:, b, :], ident[:],
-                                     start=(r == 0 and b == 0), stop=(r == TOP - 2 and b == BLOCKS - 1), is_transpose=True)
-            partial.append(total)
+                scaled = pick_and_scale(h, r)
+                if behind is not None:
+                    add_up(*behind)
+                behind = (h, r, scaled)
+        add_up(*behind)
         last = keep.tile([P, T], F32, name="last")
         nc.vector.tensor_tensor(last[:], y[:].indirect(pos_sb[TOP - 1][:]), gate_last[:], MULT)
         for h in range(2):

from contextlib import ExitStack

import concourse.mybir as mybir
from concourse.masks import make_identity

K, T, E, C, N, M = 512, 768, 12, 256, 128, 512
TOP = 4
S = E * C

FLOPS = 2 * M * K * T + 2 * K * N * S

F32 = mybir.dt.float32
BF16 = mybir.dt.bfloat16
U32 = mybir.dt.uint32
U16 = mybir.dt.uint16
U8 = mybir.dt.uint8
FP8X4 = mybir.dt.float8_e4m3fn_x4
COPY = mybir.ActivationFunctionType.Copy
MULT = mybir.AluOpType.mult
ADD = mybir.AluOpType.add

P = 128
PACK = 4
TOKEN_CHUNKS = (256, 256, 256)
SLOT_CHUNKS = (512, 512, 512, 512, 512, 256, 128, 128)
HALF = T // 2
BLOCKS = HALF // P


def starts(widths):
    return [sum(widths[:i]) for i in range(len(widths))]


def tile_moe_prv_lin_none_kernel(tc, uT, wu, w, gate, offs, pos1, pos2, pos3, pos4, out):
    nc = tc.nc
    with ExitStack() as ctx:
        lists = ctx.enter_context(tc.tile_pool(name="lists", bufs=1))
        keep = ctx.enter_context(tc.tile_pool(name="keep", bufs=1))
        ring = ctx.enter_context(tc.tile_pool(name="ring", bufs=2))
        banks = ctx.enter_context(tc.psum_pool(name="banks", bufs=4))
        sums = ctx.enter_context(tc.psum_pool(name="sums", bufs=2))
        turns = ctx.enter_context(tc.psum_pool(name="turns", bufs=2))

        def quantize(pool, grouped, width, name, tag=""):
            codes = pool.tile([P, width], U32, name=name + "_codes", tag=tag, align_bytes=64)
            scales = pool.tile([P, width], U8, name=name + "_scales", align_bytes=64)
            nc.vector.quantize_mx(out=codes[:].bitcast(FP8X4), scales=scales[:], in_=grouped)
            return codes, scales

        def multiply(result, stationary, m_cols, moving, n_cols):
            nc.tensor.matmul_mx(
                out=result,
                lhsT=stationary[0][:, m_cols].bitcast(FP8X4),
                lhsT_scale=stationary[1][:, m_cols],
                rhs=moving[0][:, n_cols].bitcast(FP8X4),
                rhs_scale=moving[1][:, n_cols],
                start=True,
                stop=True,
            )

        wu_raw = keep.tile([P, PACK, K], F32, name="wu_raw")
        nc.sync.dma_start(out=wu_raw[:], in_=wu.rearrange("(p j) c -> p j c", j=PACK))
        u_raw = []
        for t0, width in zip(starts(TOKEN_CHUNKS), TOKEN_CHUNKS):
            raw = keep.tile([P, PACK, width], F32, name=f"u_raw{t0}")
            nc.sync.dma_start(out=raw[:], in_=uT[:, t0:t0 + width].rearrange("(p j) c -> p j c", j=PACK))
            u_raw.append(raw)
        offs_sb = lists.tile([P, S // 16], U16, name="offs_sb")
        nc.sync.dma_start(offs_sb[:], offs)
        w_raw = []
        for q in range(E // 2):
            raw = keep.tile([P, 2, PACK * N], F32, name=f"w_raw{q}")
            nc.sync.dma_start(out=raw[:], in_=w[2 * q:2 * q + 2].rearrange("e (p j) n -> p e (j n)", j=PACK))
            w_raw.append(raw)
        pos_sb = []
        for r, pos in enumerate((pos1, pos2, pos3, pos4)):
            tile = lists.tile([P, T // 16], U16, name=f"pos_sb{r}")
            nc.sync.dma_start(tile[:], pos)
            pos_sb.append(tile)
        gate_last = keep.tile([P, T], F32, name="gate_last")
        nc.sync.dma_start(out=gate_last[:], in_=gate[TOP - 1])
        ident = keep.tile([P, P], F32, name="ident")
        make_identity(nc, ident[:])
        gate_rows = keep.tile([P, TOP - 1, P], F32, name="gate_rows")
        nc.gpsimd.memset(gate_rows[:], 0.0)
        nc.sync.dma_start(out=gate_rows[0:T // P, :, :], in_=gate[0:TOP - 1, 0, :].rearrange("r (c t) -> c r t", t=P))

        wu_grouped = keep.tile([P, K * PACK], BF16, name="wu_grouped", tag="staged", align_bytes=64)
        wu_view = wu_grouped[:].rearrange("p (t m j) -> p m t j", t=PACK, j=PACK)
        wu_from = wu_raw[:].rearrange("p j (m t) -> p m t j", t=PACK)
        nc.vector.tensor_copy(wu_view[:, 0:64], wu_from[:, 0:64])
        nc.scalar.activation(wu_view[:, 64:128], wu_from[:, 64:128], COPY)
        wu_mx = quantize(keep, wu_grouped[:], K, "wu")

        x_pairs = [keep.tile([P, 2 * T], BF16, name=f"x_pairs{u}", align_bytes=64) for u in range(2)]
        on_vector, on_scalar = nc.vector.tensor_copy, nc.scalar.copy

        def cast_tokens(t0, width, copies, tag):
            raw, c0 = u_raw[t0 // 256], t0 % 256
            grouped = keep.tile([P, width * PACK], BF16, name=f"u_grouped{t0}", tag=tag, align_bytes=64)
            to_view = grouped[:].rearrange("p (c i j) -> p c j i", i=4, j=PACK)
            from_view = raw[:, :, c0:c0 + width].rearrange("p j (c i) -> p c j i", i=4)
            share = width // 4 // len(copies)
            for n, copy in enumerate(copies):
                copy(to_view[:, n * share:(n + 1) * share], from_view[:, n * share:(n + 1) * share])
            return grouped

        def project(t0, width, u_mx, u, copy):
            bank = banks.tile([P, 2, width], F32, name="bank")
            for e in range(2):
                j = 2 * u + e
                multiply(bank[:, e, :], wu_mx, slice(j * P, (j + 1) * P), u_mx, slice(0, width))
            copy(
                x_pairs[u][:, 2 * t0:2 * (t0 + width)].rearrange("p (t e) -> p t e", e=2),
                bank[:].rearrange("p e t -> p t e"),
            )

        g0 = cast_tokens(0, 256, [on_scalar], "staged2")
        g1 = cast_tokens(256, 256, [on_vector, on_scalar], "staged")
        mx0 = quantize(keep, g0[:], 256, "u0")
        g2 = cast_tokens(512, 128, [on_scalar], "staged2")
        mx1 = quantize(keep, g1[:], 256, "u1")
        g3 = cast_tokens(640, 128, [on_vector], "staged")
        mx2 = quantize(keep, g2[:], 128, "u2")
        mx3 = quantize(keep, g3[:], 128, "u3", tag="late")
        pieces = ((0, 256, mx0), (256, 256, mx1), (512, 128, mx2), (640, 128, mx3))
        for piece, copy in zip(pieces, (on_scalar, on_scalar, on_vector, on_vector)):
            project(*piece, 0, copy)
        for piece in pieces:
            project(*piece, 1, on_scalar)

        y = keep.tile([P, S], F32, name="y")
        w_grouped = {}
        w_mx = {}

        def cast_weights(q):
            grouped = keep.tile([P, 2 * N * PACK], BF16, name=f"w_grouped{q}", tag="late" if q == 0 else "", align_bytes=64)
            nc.scalar.copy(
                grouped[:].rearrange("p (e c i j) -> p e c j i", e=2, i=4, j=PACK),
                w_raw[q][:].rearrange("p e (j c i) -> p e c j i", j=PACK, i=4),
            )
            w_grouped[q] = grouped

        def gather_slots(s0, width):
            planes = ring.tile([P, 2, width], U32, name="planes")
            for u in range(2):
                nc.vector.tensor_copy(
                    planes[:, u, :],
                    x_pairs[u][:].bitcast(U32).indirect(offs_sb[:, s0 // 16:(s0 + width) // 16]),
                )
            grouped = ring.tile([P, width * PACK], BF16, name="x_grouped", align_bytes=64)
            nc.scalar.copy(
                grouped[:].bitcast(U32).rearrange("p (s u) -> p s u", u=2),
                planes[:].rearrange("p u s -> p s u"),
            )
            return grouped

        def gather_slots_stepped(s0, width):
            grouped = ring.tile([P, width * PACK], BF16, name="x_grouped", align_bytes=64)
            words = grouped[:].bitcast(U32).rearrange("p (s u) -> p s u", u=2)
            for u in range(2):
                nc.vector.tensor_copy(
                    words[:, :, u],
                    x_pairs[u][:].bitcast(U32).indirect(offs_sb[:, s0 // 16:(s0 + width) // 16]),
                )
            return grouped

        def run_experts(grouped, s0, width):
            q = s0 // (2 * C)
            if q not in w_mx:
                w_mx[q] = quantize(keep, w_grouped[q][:], 2 * N, f"w{q}")
            x_mx = quantize(ring, grouped[:], width, "x")
            bank = banks.tile([P, width], F32, name="bank")
            step = min(C, width)
            for c0 in range(0, width, step):
                e = (s0 + c0) // C - 2 * q
                multiply(bank[:, c0:c0 + step], w_mx[q], slice(e * N, (e + 1) * N), x_mx, slice(c0, c0 + step))
            nc.scalar.copy(y[:, s0:s0 + width], bank[:])

        cast_weights(0)
        waiting = None
        for s0, width in zip(starts(SLOT_CHUNKS), SLOT_CHUNKS):
            grouped = (gather_slots if s0 + width < S else gather_slots_stepped)(s0, width)
            q_next = (s0 + width) // (2 * C)
            if q_next < E // 2 and q_next not in w_grouped:
                cast_weights(q_next)
            if waiting is not None:
                run_experts(*waiting)
            waiting = (grouped, s0, width)
        run_experts(*waiting)

        gate_bank = banks.tile([P, TOP - 1, P], F32, name="bank")
        for r in range(TOP - 1):
            nc.tensor.transpose(gate_bank[:, r, :], gate_rows[:, r, :], ident[:])
        gate_cols = keep.tile([P, TOP - 1, T // P], F32, name="gate_cols")
        nc.scalar.copy(gate_cols[:], gate_bank[:, :, 0:T // P])

        partial = [sums.tile([P, HALF], F32, name="total") for h in range(2)]

        def pick_and_scale(h, r):
            picked = keep.tile([P, HALF], F32, name=f"picked{h}_{r}")
            nc.vector.tensor_copy(picked[:], y[:].indirect(pos_sb[r][:, h * HALF // 16:(h + 1) * HALF // 16]))
            turned = turns.tile([P, BLOCKS, P], F32, name="turned")
            for b in range(BLOCKS):
                nc.tensor.transpose(turned[:, b, :], picked[:, b * P:(b + 1) * P], ident[:])
            scaled = keep.tile([P, BLOCKS, P], F32, name=f"scaled{h}_{r}")
            for b in range(BLOCKS):
                c = h * BLOCKS + b
                nc.scalar.activation(scaled[:, b, :], turned[:, b, :], COPY, scale=gate_cols[:, r, c:c + 1])
            return scaled

        def add_up(h, r, scaled):
            for b in range(BLOCKS):
                nc.tensor.matmul(partial[h][:, b * P:(b + 1) * P], scaled[:, b, :], ident[:],
                                 start=(r == 0 and b == 0), stop=(r == TOP - 2 and b == BLOCKS - 1), is_transpose=True)

        behind = None
        for h in range(2):
            for r in range(TOP - 1):
                scaled = pick_and_scale(h, r)
                if behind is not None:
                    add_up(*behind)
                behind = (h, r, scaled)
        add_up(*behind)
        last = keep.tile([P, T], F32, name="last")
        nc.vector.tensor_tensor(last[:], y[:].indirect(pos_sb[TOP - 1][:]), gate_last[:], MULT)
        for h in range(2):
            cols = slice(h * HALF, (h + 1) * HALF)
            result = keep.tile([P, HALF], F32, name=f"result{h}")
            nc.vector.tensor_tensor(result[:], partial[h][:], last[:, cols], ADD)
            nc.sync.dma_start(out=out[:, cols], in_=result[:])
